import numpy as np
import ml_dtypes


def mxq(x, axis, fmt="e4m3"):
    dtype, down = {"e4m3": (ml_dtypes.float8_e4m3fn, 7), "e5m2": (ml_dtypes.float8_e5m2, 14)}[fmt]
    v = np.moveaxis(np.asarray(x, np.float32).astype(ml_dtypes.bfloat16).astype(np.float64), axis, -1)
    blocks = v.reshape(v.shape[:-1] + (-1, 32))
    amax = np.abs(blocks).max(-1, keepdims=True)
    byte = np.maximum(np.where(amax > 0, np.frexp(amax)[1] - 1 + 127, 0) - down, 1)
    scale = np.exp2(byte - 127.0)
    codes = (blocks / scale).astype(np.float32).astype(dtype).astype(np.float64)
    return np.moveaxis((codes * scale).reshape(v.shape), -1, axis)


WIDE = False


def mx_kscale(k):
    if not WIDE:
        return np.ones(k)
    levels = np.array([10, -10, 5, -5, 0])
    if k % 512:
        return np.exp2(np.random.permutation(np.resize(levels, k // 32))).repeat(32)
    a = np.empty((k // 512, 16))
    for p in range(k // 512):
        a[p, :8] = np.random.permutation(np.resize(levels, 8))
        for g in range(8):
            far = levels[np.abs(levels - a[p, g]) >= 10]
            a[p, g + 8] = far[np.random.randint(len(far))]
    return np.exp2(a.ravel()).repeat(32)


def f64(x):
    return np.asarray(x).astype(np.float64)


def striped(idx):
    return np.tile(np.asarray(idx).reshape(-1, 16).T, (8, 1)).astype(np.uint16)


def unstriped(offs):
    return offs[:16].T.reshape(-1).astype(np.int64)


def striped8(idx):
    return np.asarray(idx).reshape(8, -1, 16).transpose(0, 2, 1).reshape(128, -1).astype(np.uint16)


def unstriped8(offs):
    return offs.reshape(8, 16, -1).transpose(0, 2, 1).reshape(8, -1).astype(np.int64)


def pick8(x, idx, run):
    r = np.arange(len(x))
    return x[r[:, None], idx[r % (8 * run) // run]]


E2M1 = np.array([0.0, 0.5, 1.0, 1.5, 2.0, 3.0, 4.0, 6.0, -0.0, -0.5, -1.0, -1.5, -2.0, -3.0, -4.0, -6.0])


def pack_weight(w, fmt):
    k, n = w.shape
    w = f64(np.asarray(w, np.float32).astype(ml_dtypes.bfloat16)).reshape(k // 32, 32, n)
    amax = np.abs(w).max(1)
    if fmt == "e4m3":
        byte = np.frexp(amax)[1] - 1 + 127 - 7
    else:
        mant, ex = np.frexp(amax / 6.0)
        byte = np.where(mant > 0.5, ex, ex - 1) + 127
    byte = np.clip(np.where(amax > 0, byte, 1), 1, 254)
    scaled = (w * np.exp2(127.0 - byte)[:, None, :]).reshape(k, n).astype(np.float32)
    by_word = np.ascontiguousarray(scaled.reshape(k // 512, 128, 4, n).transpose(0, 1, 3, 2))
    if fmt == "e4m3":
        words = by_word.astype(ml_dtypes.float8_e4m3fn).view(np.uint8)
    else:
        c = by_word.astype(ml_dtypes.float4_e2m1fn).view(np.uint8) & 0xF
        words = (c[..., 0::2] | (c[..., 1::2] << 4)).reshape(k // 512, 128, 2 * n)
    return np.ascontiguousarray(words), np.ascontiguousarray(byte.astype(np.uint8).reshape(k // 512, 16, n))


def unpack_weight(words, scales, fmt):
    g, _, n = scales.shape
    words = np.ascontiguousarray(words).reshape(g, 128, n, -1)
    if fmt == "e4m3":
        vals = words.view(ml_dtypes.float8_e4m3fn).astype(np.float64)
    else:
        nib = np.empty((g, 128, n, 4), np.uint8)
        nib[..., 0::2] = words & 0xF
        nib[..., 1::2] = words >> 4
        vals = E2M1[nib]
    vals = vals * np.repeat(np.exp2(scales.astype(np.float64) - 127.0), 8, axis=1)[..., None]
    return vals.transpose(0, 1, 3, 2).reshape(g * 512, n)


K, R, F, T, J, U = 512, 128, 512, 2048, 512, 1024


def setup_inputs():
    n = np.random.standard_normal
    idx = np.random.permutation(T)[:J]
    idx2 = np.stack([np.random.permutation(U)[:J] for _ in range(8)])
    fk = mx_kscale(K)
    ff = mx_kscale(F)
    tabp = pack_weight(n((K, T)) / fk[:, None], "e2m1")
    dtabp = pack_weight(n((K, T)) / fk[:, None], "e2m1")
    return {
        "tab_words": tabp[0],
        "tab_scales": tabp[1],
        "w1": (n((K, R)) * 1 / np.sqrt(K) * fk[:, None]).astype(np.float32),
        "gain": (np.random.uniform(0.5, 1.5, (R, 1))).astype(np.float32),
        "ground": (n((R, U)) * 0.7).astype(np.float32),
        "wo": (n((F, R)) * 1 / np.sqrt(F) * ff[:, None]).astype(np.float32),
        "dy": (n((F, U)) / ff[:, None]).astype(np.float32),
        "dtab_words": dtabp[0],
        "dtab_scales": dtabp[1],
        "og": (np.random.uniform(0.7, 2.0, (R, 1))).astype(np.float32),
        "base": (0.3 * n((R, J))).astype(np.float32),
        "offs": striped(idx),
        "offs2": striped8(idx2),
    }


def reference(tab_words, tab_scales, w1, gain, ground, wo, dy, dtab_words, dtab_scales, og, base, offs, offs2):
    idx = unstriped(offs)
    idx2 = unstriped8(offs2)
    tabu = unpack_weight(tab_words, tab_scales, "e2m1")
    dtabu = unpack_weight(dtab_words, dtab_scales, "e2m1")
    w1q = mxq(f64(w1), 0, "e4m3")
    tabidxg = tabu[:, idx]
    a = w1q.T @ tabidxg
    dtabidxg = dtabu[:, idx]
    ta = w1q.T @ dtabidxg
    h1 = a * f64(gain)
    pg = np.zeros((R, U))
    pg[np.arange(R)[:, None], idx2[np.arange(R) % 128 // 16]] = h1
    s = pg + f64(ground)
    u1 = np.tanh(s)
    woq = mxq(f64(wo), 0, "e4m3")
    dyq = mxq(f64(dy), 0, "e4m3")
    c0 = woq.T @ dyq
    xh1 = ta * f64(gain)
    xpg = np.zeros((R, U))
    xpg[np.arange(R)[:, None], idx2[np.arange(R) % 128 // 16]] = xh1
    xs = xpg
    xu1 = xs * (1.0 - np.square(u1))
    xds = xu1 * u1 * 2.0 * (-1.0) * c0
    xdh1 = pick8(xds, idx2, 16)
    xda = xdh1 * f64(gain)
    y = xda * f64(og) + f64(base)
    return y

@@ -1,0 +1,176 @@
+from contextlib import ExitStack
+
+import concourse.mybir as mybir
+from concourse.masks import make_identity
+
+K, R, F, T, J, U = 512, 128, 512, 2048, 512, 1024
+FLOPS = 2 * K * R * J * 2 + 2 * F * R * U
+
+F32 = mybir.dt.float32
+BF16 = mybir.dt.bfloat16
+I32 = mybir.dt.int32
+U32 = mybir.dt.uint32
+U16 = mybir.dt.uint16
+U8 = mybir.dt.uint8
+FP8X4 = mybir.dt.float8_e4m3fn_x4
+FP4X4 = mybir.dt.float4_e2m1fn_x4
+ALU = mybir.AluOpType
+ACT = mybir.ActivationFunctionType
+
+P = 128
+PACK = 4
+BANK = 512
+HALVES = U // BANK
+BLOCKS = BANK // P
+
+
+def tile_attend_hvpageput_kernel(tc, tab_words, tab_scales, w1, gain, ground, wo, dy,
+                                  dtab_words, dtab_scales, og, base, offs, offs2, out):
+    nc = tc.nc
+    with ExitStack() as ctx:
+        sb = ctx.enter_context(tc.tile_pool(name="sb", bufs=1))
+        ps = ctx.enter_context(tc.psum_pool(name="ps", bufs=1))
+
+        def sbuf(name, shape, dtype):
+            return sb.tile(shape, dtype, name=name, align_bytes=64)
+
+        def bank(name, tag=None):
+            return ps.tile([P, BANK], F32, name=name, tag=tag or name)
+
+        offs_sb = sb.tile([P, J // 16], U16, name="offs_sb")
+        offs2_sb = sb.tile([P, J // 16], U16, name="offs2_sb")
+        tab_plane = sbuf("tab_plane", [P, T], U8)
+        dtab_plane = sbuf("dtab_plane", [P, T], U8)
+        tab_sb = sbuf("tab_sb", [P, T], U16)
+        dtab_sb = sbuf("dtab_sb", [P, T], U16)
+        page = sbuf("page", [P, U], F32)
+        xpage = sbuf("xpage", [P, U], F32)
+        ident = sbuf("ident", [P, P], F32)
+
+        nc.gpsimd.memset(tab_plane[:].bitcast(I32), 0)
+        warm = sbuf("warm", [P, 1], F32)
+        nc.gpsimd.memset(warm[:], 0.0)
+        nc.vector.memset(dtab_plane[:].bitcast(I32), 0)
+        nc.vector.memset(page[:], 0.0)
+        nc.vector.memset(xpage[:], 0.0)
+        make_identity(nc, ident[:])
+
+        def load_plane(plane, scales):
+            for q in range(4):
+                nc.sync.dma_start(out=plane[32 * q:32 * q + 4, :].bitcast(I32),
+                                  in_=scales[0, 4 * q:4 * q + 4, :].bitcast(I32))
+
+        gain_sb = sbuf("gain_sb", [P, 1], F32)
+        og_sb = sbuf("og_sb", [P, 1], F32)
+        w1_raw = sbuf("w1_raw", [P, PACK, R], F32)
+        wo_raw = sbuf("wo_raw", [P, PACK, R], F32)
+        dy_raw = [sbuf("dy_raw%d" % h, [P, PACK, BANK], F32) for h in range(HALVES)]
+        ground_sb = sbuf("ground_sb", [P, U], F32)
+        base_sb = sbuf("base_sb", [P, J], F32)
+
+        nc.sync.dma_start(offs_sb[:], offs)
+        load_plane(tab_plane, tab_scales)
+        nc.sync.dma_start(out=tab_sb[:].bitcast(I32), in_=tab_words[0].bitcast(I32))
+        nc.sync.dma_start(out=w1_raw[:], in_=w1.rearrange("(p t) r -> p t r", t=PACK))
+        nc.sync.dma_start(out=gain_sb[:], in_=gain)
+        load_plane(dtab_plane, dtab_scales)
+        nc.sync.dma_start(out=dtab_sb[:].bitcast(I32), in_=dtab_words[0].bitcast(I32))
+        nc.sync.dma_start(offs2_sb[:], offs2)
+        nc.sync.dma_start(out=wo_raw[:], in_=wo.rearrange("(p t) r -> p t r", t=PACK))
+        dy_rows = dy.rearrange("(p t) u -> p t u", t=PACK)
+        for h in range(HALVES):
+            nc.sync.dma_start(out=dy_raw[h][:], in_=dy_rows[:, :, h * BANK:(h + 1) * BANK])
+        nc.sync.dma_start(out=ground_sb[:], in_=ground)
+        nc.sync.dma_start(out=og_sb[:], in_=og)
+        nc.sync.dma_start(out=base_sb[:], in_=base)
+
+        def interleave(name, raw, width):
+            woven = sbuf(name + "_woven", [P, width, PACK], BF16)
+            nc.scalar.copy(out=woven[:], in_=raw[:].rearrange("p t w -> p w t"))
+            return woven
+
+        def quantize(name, woven, width):
+            codes = sbuf(name + "_codes", [P, width], U32)
+            plane = sbuf(name + "_scales", [P, width], U8)
+            nc.vector.quantize_mx(out=codes[:].bitcast(FP8X4), scales=plane[:],
+                                  in_=woven[:].rearrange("p w t -> p (w t)"))
+            return codes, plane
+
+        def gather(name, window, dtype):
+            picked = sbuf(name, [P, J], dtype)
+            nc.vector.tensor_copy(picked[:], window[:].indirect(offs_sb[:]))
+            return picked
+
+        def first_layer(name, words, plane):
+            acc = bank(name + "_acc")
+            nc.tensor.matmul_mx(out=acc[:], lhsT=w1_codes[:].bitcast(FP8X4), lhsT_scale=w1_scales[:],
+                                rhs=words[:].bitcast(FP4X4), rhs_scale=plane[:], start=True, stop=True)
+            scaled = sbuf(name + "_scaled", [P, J], F32)
+            nc.scalar.activation(out=scaled[:], in_=acc[:], func=ACT.Copy, scale=gain_sb[:])
+            return scaled
+
+        nc.scalar.activation(out=warm[:], in_=warm[:], func=ACT.Tanh)
+
+        w1_woven = interleave("w1", w1_raw, R)
+        tab_bytes = gather("tab_bytes", tab_plane, U8)
+        tab_picked = gather("tab_picked", tab_sb, U16)
+        w1_codes, w1_scales = quantize("w1", w1_woven, R)
+        h1 = first_layer("a", tab_picked, tab_bytes)
+        dtab_bytes = gather("dtab_bytes", dtab_plane, U8)
+        dtab_picked = gather("dtab_picked", dtab_sb, U16)
+        xh1 = first_layer("ta", dtab_picked, dtab_bytes)
+        nc.vector.tensor_copy(page[:].indirect(offs2_sb[:]), h1[:])
+        nc.vector.tensor_copy(xpage[:].indirect(offs2_sb[:]), xh1[:])
+
+        factor = sbuf("factor", [P, 1], F32)
+        nc.vector.tensor_scalar(factor[:], gain_sb[:], og_sb[:], 2.0, ALU.mult, ALU.mult)
+
+        wo_woven = interleave("wo", wo_raw, R)
+        dy_woven = [interleave("dy%d" % h, dy_raw[h], BANK) for h in range(HALVES)]
+
+        s_turned = [bank("s_turned%d" % h) for h in range(HALVES)]
+        for source in (ground_sb, page):
+            for h in range(HALVES):
+                for b in range(BLOCKS):
+                    cols = slice(h * BANK + b * P, h * BANK + (b + 1) * P)
+                    nc.tensor.matmul(s_turned[h][:, b * P:(b + 1) * P], lhsT=source[:, cols], rhs=ident[:],
+                                     is_transpose=True,
+                                     start=(source is ground_sb and b == 0),
+                                     stop=(source is page and b == BLOCKS - 1))
+        u1 = [bank("u1_%d" % h) for h in range(HALVES)]
+        u1_sq = [sbuf("u1_sq%d" % h, [P, BANK], F32) for h in range(HALVES)]
+        for h in range(HALVES):
+            u_turned = sbuf("u_turned%d" % h, [P, BANK], F32)
+            nc.scalar.activation(out=u_turned[:], in_=s_turned[h][:], func=ACT.Tanh)
+            for b in range(BLOCKS):
+                nc.tensor.transpose(u1[h][:, b * P:(b + 1) * P], u_turned[:, b * P:(b + 1) * P], ident[:])
+        for h in range(HALVES):
+            nc.scalar.activation(out=u1_sq[h][:], in_=u1[h][:], func=ACT.Square)
+
+        wo_codes, wo_scales = quantize("wo", wo_woven, R)
+        c0 = []
+        for h in range(HALVES):
+            codes, plane = quantize("dy%d" % h, dy_woven[h], BANK)
+            acc = bank("c0_%d" % h, "s_turned%d" % h)
+            nc.tensor.matmul_mx(out=acc[:], lhsT=wo_codes[:].bitcast(FP8X4), lhsT_scale=wo_scales[:],
+                                rhs=codes[:].bitcast(FP8X4), rhs_scale=plane[:], start=True, stop=True)
+            c0.append(acc)
+
+        curve = [sbuf("curve%d" % h, [P, BANK], F32) for h in range(HALVES)]
+        slope = [sbuf("slope%d" % h, [P, BANK], F32) for h in range(HALVES)]
+        xds = sbuf("xds", [P, U], F32)
+        for h in range(HALVES):
+            nc.vector.scalar_tensor_tensor(curve[h][:], u1_sq[h][:], -1.0, u1[h][:], ALU.add, ALU.mult)
+        for h in range(HALVES):
+            nc.vector.scalar_tensor_tensor(slope[h][:], curve[h][:], factor[:], c0[h][:], ALU.mult, ALU.mult)
+        for h in range(HALVES):
+            cols = slice(h * BANK, (h + 1) * BANK)
+            nc.vector.tensor_tensor(xds[:, cols], slope[h][:], xpage[:, cols], ALU.mult)
+
+        half = J // 2
+        for h in range(2):
+            cols = slice(h * half, (h + 1) * half)
+            result = sbuf("result%d" % h, [P, half], F32)
+            nc.vector.tensor_tensor(result[:], xds[:].indirect(offs2_sb[:, h * half // 16:(h + 1) * half // 16]),
+                                    base_sb[:, cols], ALU.add)
+            nc.sync.dma_start(out=out[:, cols], in_=result[:])

@@ -22,6 +22,9 @@ PACK = 4
 BANK = 512
 HALVES = U // BANK
 BLOCKS = BANK // P
+CHUNK = 256
+CHUNKS = U // CHUNK
+RUN = 4
 
 
 def tile_attend_hvpageput_kernel(tc, tab_words, tab_scales, w1, gain, ground, wo, dy,
@@ -31,8 +34,8 @@ def tile_attend_hvpageput_kernel(tc, tab_words, tab_scales, w1, gain, ground, wo
         sb = ctx.enter_context(tc.tile_pool(name="sb", bufs=1))
         ps = ctx.enter_context(tc.psum_pool(name="ps", bufs=1))
 
-        def sbuf(name, shape, dtype):
-            return sb.tile(shape, dtype, name=name, align_bytes=64)
+        def sbuf(name, shape, dtype, tag=None):
+            return sb.tile(shape, dtype, name=name, tag=tag or name, align_bytes=64)
 
         def bank(name, tag=None):
             return ps.tile([P, BANK], F32, name=name, tag=tag or name)
@@ -48,8 +51,6 @@ def tile_attend_hvpageput_kernel(tc, tab_words, tab_scales, w1, gain, ground, wo
         ident = sbuf("ident", [P, P], F32)
 
         nc.gpsimd.memset(tab_plane[:].bitcast(I32), 0)
-        warm = sbuf("warm", [P, 1], F32)
-        nc.gpsimd.memset(warm[:], 0.0)
         nc.vector.memset(dtab_plane[:].bitcast(I32), 0)
         nc.vector.memset(page[:], 0.0)
         nc.vector.memset(xpage[:], 0.0)
@@ -64,33 +65,46 @@ def tile_attend_hvpageput_kernel(tc, tab_words, tab_scales, w1, gain, ground, wo
         og_sb = sbuf("og_sb", [P, 1], F32)
         w1_raw = sbuf("w1_raw", [P, PACK, R], F32)
         wo_raw = sbuf("wo_raw", [P, PACK, R], F32)
-        dy_raw = [sbuf("dy_raw%d" % h, [P, PACK, BANK], F32) for h in range(HALVES)]
+        dy_raw = [sbuf("dy_raw%d" % c, [P, PACK, CHUNK], F32) for c in range(CHUNKS)]
         ground_sb = sbuf("ground_sb", [P, U], F32)
         base_sb = sbuf("base_sb", [P, J], F32)
 
-        nc.sync.dma_start(offs_sb[:], offs)
-        load_plane(tab_plane, tab_scales)
-        nc.sync.dma_start(out=tab_sb[:].bitcast(I32), in_=tab_words[0].bitcast(I32))
-        nc.sync.dma_start(out=w1_raw[:], in_=w1.rearrange("(p t) r -> p t r", t=PACK))
-        nc.sync.dma_start(out=gain_sb[:], in_=gain)
-        load_plane(dtab_plane, dtab_scales)
-        nc.sync.dma_start(out=dtab_sb[:].bitcast(I32), in_=dtab_words[0].bitcast(I32))
-        nc.sync.dma_start(offs2_sb[:], offs2)
-        nc.sync.dma_start(out=wo_raw[:], in_=wo.rearrange("(p t) r -> p t r", t=PACK))
         dy_rows = dy.rearrange("(p t) u -> p t u", t=PACK)
-        for h in range(HALVES):
-            nc.sync.dma_start(out=dy_raw[h][:], in_=dy_rows[:, :, h * BANK:(h + 1) * BANK])
+
+        def load_dy(c):
+            nc.sync.dma_start(out=dy_raw[c][:], in_=dy_rows[:, :, c * CHUNK:(c + 1) * CHUNK])
+
+        nc.sync.dma_start(offs_sb[:], offs)
+        nc.sync.dma_start(out=tab_sb[:].bitcast(I32), in_=tab_words[0].bitcast(I32))
+        load_plane(tab_plane, tab_scales)
+        nc.sync.dma_start(out=w1_raw[:], in_=w1.rearrange("(p t) r -> p t r", t=PACK))
+        load_dy(0)
+        load_plane(dtab_plane, dtab_scales)
+        nc.sync.dma_start(out=gain_sb[:], in_=gain)
+        nc.sync.dma_start(out=dtab_sb[:].bitcast(I32), in_=dtab_words[0].bitcast(I32))
+        load_dy(1)
+        nc.sync.dma_start(offs2_sb[:], offs2)
         nc.sync.dma_start(out=ground_sb[:], in_=ground)
+        load_dy(2)
+        load_dy(3)
+        nc.sync.dma_start(out=wo_raw[:], in_=wo.rearrange("(p t) r -> p t r", t=PACK))
         nc.sync.dma_start(out=og_sb[:], in_=og)
         nc.sync.dma_start(out=base_sb[:], in_=base)
 
-        def interleave(name, raw, width):
-            woven = sbuf(name + "_woven", [P, width, PACK], BF16)
-            nc.scalar.copy(out=woven[:], in_=raw[:].rearrange("p t w -> p w t"))
-            return woven
+        def interleave(woven, raw):
+            nc.scalar.activation(out=woven.rearrange("p (c i) t -> p c t i", i=RUN),
+                                 in_=raw.rearrange("p t (c i) -> p c t i", i=RUN), func=ACT.Copy)
 
-        def quantize(name, woven, width):
-            codes = sbuf(name + "_codes", [P, width], U32)
+        w1_woven = sbuf("w1_woven", [P, R, PACK], BF16)
+        wo_woven = sbuf("wo_woven", [P, R, PACK], BF16)
+        dy_woven = [sbuf("dy_woven%d" % h, [P, BANK, PACK], BF16) for h in range(HALVES)]
+
+        def interleave_dy(c):
+            h, first = divmod(c * CHUNK, BANK)
+            interleave(dy_woven[h][:, first:first + CHUNK, :], dy_raw[c][:])
+
+        def quantize(name, woven, width, tag=None):
+            codes = sbuf(name + "_codes", [P, width], U32, tag)
             plane = sbuf(name + "_scales", [P, width], U8)
             nc.vector.quantize_mx(out=codes[:].bitcast(FP8X4), scales=plane[:],
                                   in_=woven[:].rearrange("p w t -> p (w t)"))
@@ -101,60 +115,59 @@ def tile_attend_hvpageput_kernel(tc, tab_words, tab_scales, w1, gain, ground, wo
             nc.vector.tensor_copy(picked[:], window[:].indirect(offs_sb[:]))
             return picked
 
-        def first_layer(name, words, plane):
+        def first_layer(name, words, plane, tag):
             acc = bank(name + "_acc")
             nc.tensor.matmul_mx(out=acc[:], lhsT=w1_codes[:].bitcast(FP8X4), lhsT_scale=w1_scales[:],
                                 rhs=words[:].bitcast(FP4X4), rhs_scale=plane[:], start=True, stop=True)
-            scaled = sbuf(name + "_scaled", [P, J], F32)
+            scaled = sbuf(name + "_scaled", [P, J], F32, tag)
             nc.scalar.activation(out=scaled[:], in_=acc[:], func=ACT.Copy, scale=gain_sb[:])
             return scaled
 
-        nc.scalar.activation(out=warm[:], in_=warm[:], func=ACT.Tanh)
-
-        w1_woven = interleave("w1", w1_raw, R)
-        tab_bytes = gather("tab_bytes", tab_plane, U8)
+        interleave(w1_woven[:], w1_raw[:])
+        interleave_dy(0)
         tab_picked = gather("tab_picked", tab_sb, U16)
+        tab_bytes = gather("tab_bytes", tab_plane, U8)
         w1_codes, w1_scales = quantize("w1", w1_woven, R)
-        h1 = first_layer("a", tab_picked, tab_bytes)
+        h1 = first_layer("a", tab_picked, tab_bytes, "dy_raw0")
+        interleave_dy(1)
         dtab_bytes = gather("dtab_bytes", dtab_plane, U8)
         dtab_picked = gather("dtab_picked", dtab_sb, U16)
-        xh1 = first_layer("ta", dtab_picked, dtab_bytes)
+        xh1 = first_layer("ta", dtab_picked, dtab_bytes, "dy_raw1")
         nc.vector.tensor_copy(page[:].indirect(offs2_sb[:]), h1[:])
         nc.vector.tensor_copy(xpage[:].indirect(offs2_sb[:]), xh1[:])
 
         factor = sbuf("factor", [P, 1], F32)
         nc.vector.tensor_scalar(factor[:], gain_sb[:], og_sb[:], 2.0, ALU.mult, ALU.mult)
 
-        wo_woven = interleave("wo", wo_raw, R)
-        dy_woven = [interleave("dy%d" % h, dy_raw[h], BANK) for h in range(HALVES)]
+        interleave_dy(2)
+        interleave_dy(3)
 
-        s_turned = [bank("s_turned%d" % h) for h in range(HALVES)]
+        s_turned = ps.tile([P, U], F32, name="s_turned", tag="wide")
         for source in (ground_sb, page):
             for h in range(HALVES):
                 for b in range(BLOCKS):
                     cols = slice(h * BANK + b * P, h * BANK + (b + 1) * P)
-                    nc.tensor.matmul(s_turned[h][:, b * P:(b + 1) * P], lhsT=source[:, cols], rhs=ident[:],
+                    nc.tensor.matmul(s_turned[:, cols], lhsT=source[:, cols], rhs=ident[:],
                                      is_transpose=True,
                                      start=(source is ground_sb and b == 0),
                                      stop=(source is page and b == BLOCKS - 1))
         u1 = [bank("u1_%d" % h) for h in range(HALVES)]
         u1_sq = [sbuf("u1_sq%d" % h, [P, BANK], F32) for h in range(HALVES)]
         for h in range(HALVES):
-            u_turned = sbuf("u_turned%d" % h, [P, BANK], F32)
-            nc.scalar.activation(out=u_turned[:], in_=s_turned[h][:], func=ACT.Tanh)
+            u_turned = sbuf("u_turned%d" % h, [P, BANK], F32, "dy_raw%d" % (CHUNKS - 1 - h))
+            nc.scalar.activation(out=u_turned[:], in_=s_turned[:, h * BANK:(h + 1) * BANK], func=ACT.Tanh)
             for b in range(BLOCKS):
                 nc.tensor.transpose(u1[h][:, b * P:(b + 1) * P], u_turned[:, b * P:(b + 1) * P], ident[:])
+        interleave(wo_woven[:], wo_raw[:])
         for h in range(HALVES):
             nc.scalar.activation(out=u1_sq[h][:], in_=u1[h][:], func=ACT.Square)
 
-        wo_codes, wo_scales = quantize("wo", wo_woven, R)
-        c0 = []
+        wo_codes, wo_scales = quantize("wo", wo_woven, R, "dy_raw%d" % (CHUNKS - HALVES))
+        c0 = ps.tile([P, U], F32, name="c0", tag="wide")
         for h in range(HALVES):
             codes, plane = quantize("dy%d" % h, dy_woven[h], BANK)
-            acc = bank("c0_%d" % h, "s_turned%d" % h)
-            nc.tensor.matmul_mx(out=acc[:], lhsT=wo_codes[:].bitcast(FP8X4), lhsT_scale=wo_scales[:],
+            nc.tensor.matmul_mx(out=c0[:, h * BANK:(h + 1) * BANK], lhsT=wo_codes[:].bitcast(FP8X4), lhsT_scale=wo_scales[:],
                                 rhs=codes[:].bitcast(FP8X4), rhs_scale=plane[:], start=True, stop=True)
-            c0.append(acc)
 
         curve = [sbuf("curve%d" % h, [P, BANK], F32) for h in range(HALVES)]
         slope = [sbuf("slope%d" % h, [P, BANK], F32) for h in range(HALVES)]
@@ -162,7 +175,7 @@ def tile_attend_hvpageput_kernel(tc, tab_words, tab_scales, w1, gain, ground, wo
         for h in range(HALVES):
             nc.vector.scalar_tensor_tensor(curve[h][:], u1_sq[h][:], -1.0, u1[h][:], ALU.add, ALU.mult)
         for h in range(HALVES):
-            nc.vector.scalar_tensor_tensor(slope[h][:], curve[h][:], factor[:], c0[h][:], ALU.mult, ALU.mult)
+            nc.vector.scalar_tensor_tensor(slope[h][:], curve[h][:], factor[:], c0[:, h * BANK:(h + 1) * BANK], ALU.mult, ALU.mult)
         for h in range(HALVES):
             cols = slice(h * BANK, (h + 1) * BANK)
             nc.vector.tensor_tensor(xds[:, cols], slope[h][:], xpage[:, cols], ALU.mult)

from contextlib import ExitStack

import concourse.mybir as mybir
from concourse.masks import make_identity

K, R, F, T, J, U = 512, 128, 512, 2048, 512, 1024
FLOPS = 2 * K * R * J * 2 + 2 * F * R * U

F32 = mybir.dt.float32
BF16 = mybir.dt.bfloat16
I32 = mybir.dt.int32
U32 = mybir.dt.uint32
U16 = mybir.dt.uint16
U8 = mybir.dt.uint8
FP8X4 = mybir.dt.float8_e4m3fn_x4
FP4X4 = mybir.dt.float4_e2m1fn_x4
ALU = mybir.AluOpType
ACT = mybir.ActivationFunctionType

P = 128
PACK = 4
BANK = 512
HALVES = U // BANK
BLOCKS = BANK // P
CHUNK = 256
CHUNKS = U // CHUNK
RUN = 4


def tile_attend_hvpageput_kernel(tc, tab_words, tab_scales, w1, gain, ground, wo, dy,
                                  dtab_words, dtab_scales, og, base, offs, offs2, out):
    nc = tc.nc
    with ExitStack() as ctx:
        sb = ctx.enter_context(tc.tile_pool(name="sb", bufs=1))
        ps = ctx.enter_context(tc.psum_pool(name="ps", bufs=1))

        def sbuf(name, shape, dtype, tag=None):
            return sb.tile(shape, dtype, name=name, tag=tag or name, align_bytes=64)

        def bank(name, tag=None):
            return ps.tile([P, BANK], F32, name=name, tag=tag or name)

        offs_sb = sb.tile([P, J // 16], U16, name="offs_sb")
        offs2_sb = sb.tile([P, J // 16], U16, name="offs2_sb")
        tab_plane = sbuf("tab_plane", [P, T], U8)
        dtab_plane = sbuf("dtab_plane", [P, T], U8)
        tab_sb = sbuf("tab_sb", [P, T], U16)
        dtab_sb = sbuf("dtab_sb", [P, T], U16)
        page = sbuf("page", [P, U], F32)
        xpage = sbuf("xpage", [P, U], F32)
        ident = sbuf("ident", [P, P], F32)

        nc.gpsimd.memset(tab_plane[:].bitcast(I32), 0)
        nc.vector.memset(dtab_plane[:].bitcast(I32), 0)
        nc.vector.memset(page[:], 0.0)
        nc.vector.memset(xpage[:], 0.0)
        make_identity(nc, ident[:])

        def load_plane(plane, scales):
            for q in range(4):
                nc.sync.dma_start(out=plane[32 * q:32 * q + 4, :].bitcast(I32),
                                  in_=scales[0, 4 * q:4 * q + 4, :].bitcast(I32))

        gain_sb = sbuf("gain_sb", [P, 1], F32)
        og_sb = sbuf("og_sb", [P, 1], F32)
        w1_raw = sbuf("w1_raw", [P, PACK, R], F32)
        wo_raw = sbuf("wo_raw", [P, PACK, R], F32)
        dy_raw = [sbuf("dy_raw%d" % c, [P, PACK, CHUNK], F32) for c in range(CHUNKS)]
        ground_sb = sbuf("ground_sb", [P, U], F32)
        base_sb = sbuf("base_sb", [P, J], F32)

        dy_rows = dy.rearrange("(p t) u -> p t u", t=PACK)

        def load_dy(c):
            nc.sync.dma_start(out=dy_raw[c][:], in_=dy_rows[:, :, c * CHUNK:(c + 1) * CHUNK])

        nc.sync.dma_start(offs_sb[:], offs)
        nc.sync.dma_start(out=tab_sb[:].bitcast(I32), in_=tab_words[0].bitcast(I32))
        load_plane(tab_plane, tab_scales)
        nc.sync.dma_start(out=w1_raw[:], in_=w1.rearrange("(p t) r -> p t r", t=PACK))
        load_dy(0)
        load_plane(dtab_plane, dtab_scales)
        nc.sync.dma_start(out=gain_sb[:], in_=gain)
        nc.sync.dma_start(out=dtab_sb[:].bitcast(I32), in_=dtab_words[0].bitcast(I32))
        load_dy(1)
        nc.sync.dma_start(offs2_sb[:], offs2)
        nc.sync.dma_start(out=ground_sb[:], in_=ground)
        load_dy(2)
        load_dy(3)
        nc.sync.dma_start(out=wo_raw[:], in_=wo.rearrange("(p t) r -> p t r", t=PACK))
        nc.sync.dma_start(out=og_sb[:], in_=og)
        nc.sync.dma_start(out=base_sb[:], in_=base)

        def interleave(woven, raw):
            nc.scalar.activation(out=woven.rearrange("p (c i) t -> p c t i", i=RUN),
                                 in_=raw.rearrange("p t (c i) -> p c t i", i=RUN), func=ACT.Copy)

        w1_woven = sbuf("w1_woven", [P, R, PACK], BF16)
        wo_woven = sbuf("wo_woven", [P, R, PACK], BF16)
        dy_woven = [sbuf("dy_woven%d" % h, [P, BANK, PACK], BF16) for h in range(HALVES)]

        def interleave_dy(c):
            h, first = divmod(c * CHUNK, BANK)
            interleave(dy_woven[h][:, first:first + CHUNK, :], dy_raw[c][:])

        def quantize(name, woven, width, tag=None):
            codes = sbuf(name + "_codes", [P, width], U32, tag)
            plane = sbuf(name + "_scales", [P, width], U8)
            nc.vector.quantize_mx(out=codes[:].bitcast(FP8X4), scales=plane[:],
                                  in_=woven[:].rearrange("p w t -> p (w t)"))
            return codes, plane

        def gather(name, window, dtype):
            picked = sbuf(name, [P, J], dtype)
            nc.vector.tensor_copy(picked[:], window[:].indirect(offs_sb[:]))
            return picked

        def first_layer(name, words, plane, tag):
            acc = bank(name + "_acc")
            nc.tensor.matmul_mx(out=acc[:], lhsT=w1_codes[:].bitcast(FP8X4), lhsT_scale=w1_scales[:],
                                rhs=words[:].bitcast(FP4X4), rhs_scale=plane[:], start=True, stop=True)
            scaled = sbuf(name + "_scaled", [P, J], F32, tag)
            nc.scalar.activation(out=scaled[:], in_=acc[:], func=ACT.Copy, scale=gain_sb[:])
            return scaled

        interleave(w1_woven[:], w1_raw[:])
        interleave_dy(0)
        tab_picked = gather("tab_picked", tab_sb, U16)
        tab_bytes = gather("tab_bytes", tab_plane, U8)
        w1_codes, w1_scales = quantize("w1", w1_woven, R)
        h1 = first_layer("a", tab_picked, tab_bytes, "dy_raw0")
        interleave_dy(1)
        dtab_bytes = gather("dtab_bytes", dtab_plane, U8)
        dtab_picked = gather("dtab_picked", dtab_sb, U16)
        xh1 = first_layer("ta", dtab_picked, dtab_bytes, "dy_raw1")
        nc.vector.tensor_copy(page[:].indirect(offs2_sb[:]), h1[:])
        nc.vector.tensor_copy(xpage[:].indirect(offs2_sb[:]), xh1[:])

        factor = sbuf("factor", [P, 1], F32)
        nc.vector.tensor_scalar(factor[:], gain_sb[:], og_sb[:], 2.0, ALU.mult, ALU.mult)

        interleave_dy(2)
        interleave_dy(3)

        s_turned = ps.tile([P, U], F32, name="s_turned", tag="wide")
        for source in (ground_sb, page):
            for h in range(HALVES):
                for b in range(BLOCKS):
                    cols = slice(h * BANK + b * P, h * BANK + (b + 1) * P)
                    nc.tensor.matmul(s_turned[:, cols], lhsT=source[:, cols], rhs=ident[:],
                                     is_transpose=True,
                                     start=(source is ground_sb and b == 0),
                                     stop=(source is page and b == BLOCKS - 1))
        u1 = [bank("u1_%d" % h) for h in range(HALVES)]
        u1_sq = [sbuf("u1_sq%d" % h, [P, BANK], F32) for h in range(HALVES)]
        for h in range(HALVES):
            u_turned = sbuf("u_turned%d" % h, [P, BANK], F32, "dy_raw%d" % (CHUNKS - 1 - h))
            nc.scalar.activation(out=u_turned[:], in_=s_turned[:, h * BANK:(h + 1) * BANK], func=ACT.Tanh)
            for b in range(BLOCKS):
                nc.tensor.transpose(u1[h][:, b * P:(b + 1) * P], u_turned[:, b * P:(b + 1) * P], ident[:])
        interleave(wo_woven[:], wo_raw[:])
        for h in range(HALVES):
            nc.scalar.activation(out=u1_sq[h][:], in_=u1[h][:], func=ACT.Square)

        wo_codes, wo_scales = quantize("wo", wo_woven, R, "dy_raw%d" % (CHUNKS - HALVES))
        c0 = ps.tile([P, U], F32, name="c0", tag="wide")
        for h in range(HALVES):
            codes, plane = quantize("dy%d" % h, dy_woven[h], BANK)
            nc.tensor.matmul_mx(out=c0[:, h * BANK:(h + 1) * BANK], lhsT=wo_codes[:].bitcast(FP8X4), lhsT_scale=wo_scales[:],
                                rhs=codes[:].bitcast(FP8X4), rhs_scale=plane[:], start=True, stop=True)

        curve = [sbuf("curve%d" % h, [P, BANK], F32) for h in range(HALVES)]
        slope = [sbuf("slope%d" % h, [P, BANK], F32) for h in range(HALVES)]
        xds = sbuf("xds", [P, U], F32)
        for h in range(HALVES):
            nc.vector.scalar_tensor_tensor(curve[h][:], u1_sq[h][:], -1.0, u1[h][:], ALU.add, ALU.mult)
        for h in range(HALVES):
            nc.vector.scalar_tensor_tensor(slope[h][:], curve[h][:], factor[:], c0[:, h * BANK:(h + 1) * BANK], ALU.mult, ALU.mult)
        for h in range(HALVES):
            cols = slice(h * BANK, (h + 1) * BANK)
            nc.vector.tensor_tensor(xds[:, cols], slope[h][:], xpage[:, cols], ALU.mult)

        half = J // 2
        for h in range(2):
            cols = slice(h * half, (h + 1) * half)
            result = sbuf("result%d" % h, [P, half], F32)
            nc.vector.tensor_tensor(result[:], xds[:].indirect(offs2_sb[:, h * half // 16:(h + 1) * half // 16]),
                                    base_sb[:, cols], ALU.add)
            nc.sync.dma_start(out=out[:, cols], in_=result[:])
